import numpy as np
import ml_dtypes


def mxq(x, axis, fmt="e4m3"):
    dtype, down = {"e4m3": (ml_dtypes.float8_e4m3fn, 7), "e5m2": (ml_dtypes.float8_e5m2, 14)}[fmt]
    v = np.moveaxis(np.asarray(x, np.float32).astype(ml_dtypes.bfloat16).astype(np.float64), axis, -1)
    blocks = v.reshape(v.shape[:-1] + (-1, 32))
    amax = np.abs(blocks).max(-1, keepdims=True)
    byte = np.maximum(np.where(amax > 0, np.frexp(amax)[1] - 1 + 127, 0) - down, 1)
    scale = np.exp2(byte - 127.0)
    codes = (blocks / scale).astype(np.float32).astype(dtype).astype(np.float64)
    return np.moveaxis((codes * scale).reshape(v.shape), -1, axis)


WIDE = False


def mx_kscale(k):
    if not WIDE:
        return np.ones(k)
    levels = np.array([10, -10, 5, -5, 0])
    if k % 512:
        return np.exp2(np.random.permutation(np.resize(levels, k // 32))).repeat(32)
    a = np.empty((k // 512, 16))
    for p in range(k // 512):
        a[p, :8] = np.random.permutation(np.resize(levels, 8))
        for g in range(8):
            far = levels[np.abs(levels - a[p, g]) >= 10]
            a[p, g + 8] = far[np.random.randint(len(far))]
    return np.exp2(a.ravel()).repeat(32)


def f64(x):
    return np.asarray(x).astype(np.float64)


def striped(idx):
    return np.tile(idx.reshape(-1, 16).T, (8, 1)).astype(np.uint16)


def unstriped(offs):
    return offs[:16].T.reshape(-1).astype(np.int64)


E2M1 = np.array([0.0, 0.5, 1.0, 1.5, 2.0, 3.0, 4.0, 6.0, -0.0, -0.5, -1.0, -1.5, -2.0, -3.0, -4.0, -6.0])


def pack_weight(w, fmt):
    k, n = w.shape
    w = f64(np.asarray(w, np.float32).astype(ml_dtypes.bfloat16)).reshape(k // 32, 32, n)
    amax = np.abs(w).max(1)
    if fmt == "e4m3":
        byte = np.frexp(amax)[1] - 1 + 127 - 7
    else:
        mant, ex = np.frexp(amax / 6.0)
        byte = np.where(mant > 0.5, ex, ex - 1) + 127
    byte = np.clip(np.where(amax > 0, byte, 1), 1, 254)
    scaled = (w * np.exp2(127.0 - byte)[:, None, :]).reshape(k, n).astype(np.float32)
    by_word = np.ascontiguousarray(scaled.reshape(k // 512, 128, 4, n).transpose(0, 1, 3, 2))
    if fmt == "e4m3":
        words = by_word.astype(ml_dtypes.float8_e4m3fn).view(np.uint8)
    else:
        c = by_word.astype(ml_dtypes.float4_e2m1fn).view(np.uint8) & 0xF
        words = (c[..., 0::2] | (c[..., 1::2] << 4)).reshape(k // 512, 128, 2 * n)
    return np.ascontiguousarray(words), np.ascontiguousarray(byte.astype(np.uint8).reshape(k // 512, 16, n))


def unpack_weight(words, scales, fmt):
    g, _, n = scales.shape
    words = np.ascontiguousarray(words).reshape(g, 128, n, -1)
    if fmt == "e4m3":
        vals = words.view(ml_dtypes.float8_e4m3fn).astype(np.float64)
    else:
        nib = np.empty((g, 128, n, 4), np.uint8)
        nib[..., 0::2] = words & 0xF
        nib[..., 1::2] = words >> 4
        vals = E2M1[nib]
    vals = vals * np.repeat(np.exp2(scales.astype(np.float64) - 127.0), 8, axis=1)[..., None]
    return vals.transpose(0, 1, 3, 2).reshape(g * 512, n)


def relu2(v):
    return np.maximum(v, 0.0) ** 2


K, T, E, C, H, N = 1536, 2048, 6, 256, 512, 384


def by_expert(wq, xq):
    return np.concatenate([wq[e].T @ xq[:, e * C:(e + 1) * C] for e in range(E)], axis=1)


def setup_inputs():
    n = np.random.standard_normal
    s = mx_kscale(K)[:, None]
    u = mx_kscale(H)
    w1 = [pack_weight(m, "e2m1") for m in n((E, K, H)) / np.sqrt(K) / s[None] * u[None, None, :]]
    w2 = [pack_weight(m, "e2m1") for m in n((E, H, N)) / np.sqrt(H) / u[None, :, None] ** 2]
    x = pack_weight(n((K, T)) * s, "e4m3")
    return {
        "x_words": x[0],
        "x_scales": x[1],
        "w1_words": np.stack([m[0] for m in w1]),
        "w1_scales": np.stack([m[1] for m in w1]),
        "w2_words": np.stack([m[0] for m in w2]),
        "w2_scales": np.stack([m[1] for m in w2]),
        "gate": np.tile(np.random.uniform(0.2, 1.0, E * C), (N, 1)).astype(np.float32),
        "offs": striped(np.random.permutation(T)[:E * C]),
    }


def reference(x_words, x_scales, w1_words, w1_scales, w2_words, w2_scales, gate, offs):
    idx = unstriped(offs)
    w1 = np.stack([unpack_weight(w1_words[e], w1_scales[e], "e2m1") for e in range(E)])
    w2 = np.stack([unpack_weight(w2_words[e], w2_scales[e], "e2m1") for e in range(E)])
    xq = unpack_weight(x_words, x_scales, "e4m3")[:, idx]
    h = relu2(by_expert(w1, xq))
    y = by_expert(w2, mxq(h, 0, "e4m3"))
    out = np.zeros((N, T))
    out[:, idx] = f64(gate) * y
    return out

@@ -1,0 +1,235 @@
+from contextlib import ExitStack
+
+import concourse.mybir as mybir
+from concourse.masks import make_identity
+
+K, T, E, C, H, N = 1536, 2048, 6, 256, 512, 384
+S = E * C
+P = 128
+PASSES = K // 512
+BLOCKS = N // P
+FLOPS = 2 * S * (K * H + H * N)
+
+F32 = mybir.dt.float32
+BF16 = mybir.dt.bfloat16
+I32 = mybir.dt.int32
+U32 = mybir.dt.uint32
+U16 = mybir.dt.uint16
+U8 = mybir.dt.uint8
+FP8X4 = mybir.dt.float8_e4m3fn_x4
+FP4X4 = mybir.dt.float4_e2m1fn_x4
+ACT = mybir.ActivationFunctionType
+MULT = mybir.AluOpType.mult
+
+ROW0 = P - 16 * PASSES
+W1_GROUPS = ((0, 1), (1, 3), (3, 6))
+
+
+def tile_moe_pkd_mlp_relu2_kernel(
+    tc, x_words, x_scales, w1_words, w1_scales, w2_words, w2_scales, gate, offs, out
+):
+    nc = tc.nc
+    with ExitStack() as ctx:
+        keep = ctx.enter_context(tc.tile_pool(name="keep", bufs=1))
+        ring = ctx.enter_context(tc.tile_pool(name="ring", bufs=2))
+        psum = ctx.enter_context(tc.psum_pool(name="psum", bufs=1))
+
+        offsets = keep.tile([P, S // 16], U16, name="offsets")
+        nc.sync.dma_start(offsets[:], offs)
+
+        def listed(a, b):
+            return offsets[:, a // 16 : b // 16]
+
+        w1s = [keep.tile([P, (b - a) * PASSES, H], U8, name="w1s%d" % a, align_bytes=64) for a, b in W1_GROUPS[:2]]
+        xs = keep.tile([P, T], U8, name="xs", tag="xs", align_bytes=64)
+        planes = keep.tile([P, PASSES * S], U8, name="planes", align_bytes=64)
+        w2s = keep.tile([P, E, N], U8, name="w2s", align_bytes=64)
+        zero = keep.tile([P, 8], F32, name="zero")
+
+        def clear(t):
+            nc.vector.memset(t.bitcast(I32), 0)
+
+        clear(xs[0:ROW0, :])
+        clear(w1s[0][:])
+        nc.vector.memset(zero[:], 0.0)
+        clear(planes[:])
+        clear(w1s[1][:])
+        clear(w2s[:])
+
+        for o in range(PASSES):
+            nc.sync.dma_start(xs[ROW0 + o : P : PASSES, :].bitcast(I32), x_scales[o].bitcast(I32))
+        xw = [keep.tile([P, T], U32, name="xw%d" % o, tag="xw%d" % o, align_bytes=64) for o in range(PASSES)]
+        for o in range(PASSES):
+            nc.sync.dma_start(xw[o][:].bitcast(I32), x_words[o].rearrange("p t r -> p (t r)").bitcast(I32))
+
+        w1 = {}
+
+        def load_w1(g, tag):
+            a, b = W1_GROUPS[g]
+            w1[g] = keep.tile([P, (b - a) * PASSES, 2 * H], U8, name="w1_%d" % g, tag=tag, align_bytes=64)
+            nc.sync.dma_start(w1[g][:].bitcast(I32), w1_words[a:b].rearrange("e s p c -> p (e s) c").bitcast(I32))
+
+        def load_scales(tile, rows, queue):
+            by_row = rows.rearrange("e s (q r) i -> r q (e s) i", r=4)
+            for r in range(4):
+                queue.dma_start(tile[r:P:32, :, :].bitcast(I32), by_row[r].bitcast(I32))
+
+        def load_w1_scales(g, queue, shift=0):
+            a, b = W1_GROUPS[g]
+            load_scales(w1s[g], w1_scales[a + shift : b + shift], queue)
+
+        load_w1(0, "w1_first")
+        load_w1_scales(0, nc.gpsimd)
+        ident = keep.tile([P, P], F32, name="ident")
+        make_identity(nc, ident[:])
+        load_w1_scales(1, nc.gpsimd)
+        load_scales(w2s, w2_scales, nc.gpsimd)
+
+        picked = keep.tile([P, S], U8, name="picked", tag="picked", align_bytes=64)
+        nc.vector.tensor_copy(picked[:], xs[:].indirect(offsets[:]))
+        for q in range(4):
+            nc.scalar.dma_start(
+                planes[32 * q : 32 * q + 4, :].bitcast(I32),
+                picked[ROW0 + 12 * q : ROW0 + 12 * q + 12, :].bitcast(I32),
+            )
+
+        load_w1(1, "xs")
+        w2 = keep.tile([P, E, 2 * N], U8, name="w2", tag="picked", align_bytes=64)
+        nc.sync.dma_start(w2[:].bitcast(I32), w2_words.rearrange("e s p c -> p (e s) c").bitcast(I32))
+
+        windows = [keep.tile([P, T], F32, name="window%d" % b) for b in range(BLOCKS)]
+        for b in range(BLOCKS):
+            nc.scalar.copy(windows[b][:], zero[:, 0:1].to_broadcast([P, T]))
+
+        words = {}
+
+        def gather(tile, o, a, b):
+            nc.vector.tensor_copy(tile[:, 0 : b - a], xw[o][:].indirect(listed(a, b)))
+            for j in range(a // P, b // P):
+                words[(o, j)] = tile[:, j * P - a : (j + 1) * P - a]
+
+        shared = keep.tile([P, 2 * C], U32, name="shared", align_bytes=64)
+        g0 = keep.tile([P, S - C], U32, name="g0", align_bytes=64)
+        g1a = keep.tile([P, C], U32, name="g1a", align_bytes=64)
+        g2a = keep.tile([P, C], U32, name="g2a", align_bytes=64)
+        g2 = keep.tile([P, S - C], U32, name="g2", align_bytes=64)
+        gather(shared, 0, 0, C)
+        gather(g0, 0, C, S)
+        gates = keep.tile([P, S], F32, name="gates", tag="xw0", align_bytes=64)
+        nc.sync.dma_start(gates[:], gate[0:P, :])
+        gather(g1a, 1, 0, C)
+        gather(g2a, 2, 0, C)
+        gather(g2, 2, C, S)
+        load_w1(2, "xw2")
+
+        acc = [psum.tile([P, H], F32, name="acc%d" % n) for n in range(3)]
+        turned = [psum.tile([P, 4, P], F32, name="turned%d" % n) for n in range(4)]
+        early_bank = psum.tile([P, 2 * C], F32, name="early_bank")
+        codes = keep.tile([P, S], U32, name="codes", align_bytes=64)
+        hs = keep.tile([P, S], U8, name="hs", align_bytes=64)
+        ys = keep.tile([P, BLOCKS, S], F32, name="ys")
+        relu = {}
+        hidden = {}
+
+        def first_layer(j):
+            e = j // 2
+            g = [n for n, (a, b) in enumerate(W1_GROUPS) if a <= e < b][0]
+            first = W1_GROUPS[g][0]
+            order = (2, 0, 1)
+            for n, o in enumerate(order):
+                nc.tensor.matmul_mx(
+                    out=acc[j % 3][:],
+                    lhsT=words[(o, j)].bitcast(FP8X4),
+                    lhsT_scale=planes[:, o * S + j * P : o * S + (j + 1) * P],
+                    rhs=w1[g][:, (e - first) * PASSES + o, :].bitcast(FP4X4),
+                    rhs_scale=w1s[min(e % 3, 1)][:, max(e % 3 - 1, 0) * PASSES + o, :],
+                    start=(n == 0),
+                    stop=(n == PASSES - 1),
+                )
+            relu[j] = ring.tile([P, 4, P], F32, name="relu", bufs=3)
+            nc.scalar.activation(relu[j][:], acc[j % 3][:].rearrange("p (m t) -> p t m", t=4), ACT.Relu)
+
+        def turn(j):
+            e = j // 2
+            if j % 2 == 0:
+                if e == 0:
+                    hidden[e] = keep.tile([P, C, 4], BF16, name="hidden0", tag="handover", align_bytes=64)
+                else:
+                    hidden[e] = ring.tile([P, C, 4], BF16, name="hidden", align_bytes=64)
+            for t in range(4):
+                nc.tensor.transpose(turned[j % 4][:, t, :], relu[j][:, t, :], ident[:])
+            half = (j % 2) * P
+            nc.scalar.activation(
+                hidden[e][:, half : half + P, :], turned[j % 4][:].rearrange("p t s -> p s t"), ACT.Square
+            )
+
+        def quantise(e):
+            nc.vector.quantize_mx(
+                out=codes[:, e * C : (e + 1) * C].bitcast(FP8X4),
+                scales=hs[:, e * C : (e + 1) * C],
+                in_=hidden[e][:].rearrange("p s t -> p (s t)"),
+            )
+
+        def second_matmul(e, b, bank):
+            nc.tensor.matmul_mx(
+                out=bank,
+                lhsT=w2[:, e, 2 * b * P : 2 * (b + 1) * P].bitcast(FP4X4),
+                lhsT_scale=w2s[:, e, b * P : (b + 1) * P],
+                rhs=codes[:, e * C : (e + 1) * C].bitcast(FP8X4),
+                rhs_scale=hs[:, e * C : (e + 1) * C],
+                start=True,
+                stop=True,
+            )
+
+        def scatter(b, lo, hi):
+            nc.vector.tensor_tensor(windows[b][:].indirect(listed(lo, hi)), ys[:, b, lo:hi], gates[:, lo:hi], MULT)
+
+        def flat(bank):
+            return bank[:].rearrange("p t s -> p (t s)")
+
+        def blocks_of_expert(e, blocks, bank):
+            for u, b in enumerate(blocks):
+                second_matmul(e, b, bank[:, u * C : (u + 1) * C])
+            nc.scalar.copy(
+                ys[:, blocks[0] : blocks[-1] + 1, e * C : (e + 1) * C],
+                bank[:, 0 : len(blocks) * C].rearrange("p (u c) -> p u c", c=C),
+            )
+            for b in blocks:
+                scatter(b, e * C, (e + 1) * C)
+
+        def last_block(experts, bank):
+            for u, e in enumerate(experts):
+                second_matmul(e, 2, bank[:, u * C : (u + 1) * C])
+            nc.scalar.copy(ys[:, 2, experts[0] * C : (experts[-1] + 1) * C], bank[:, 0 : len(experts) * C])
+
+        first_layer(0)
+        first_layer(1)
+        gather(shared, 1, C, 3 * C)
+        load_w1_scales(0, nc.sync, 3)
+        for j in range(2 * E):
+            turn(j)
+            if j == 1:
+                quantise(0)
+                g1c = keep.tile([P, 3 * C], U32, name="g1c", tag="handover", align_bytes=64)
+                gather(g1c, 1, 3 * C, S)
+            if j + 2 < 2 * E:
+                first_layer(j + 2)
+            if j + 2 == 5:
+                load_w1_scales(1, nc.sync, 3)
+            if j == 1:
+                blocks_of_expert(0, (0,), early_bank[:])
+            elif j % 2 == 1:
+                e = j // 2
+                quantise(e)
+                blocks_of_expert(e - 1, (1, 2) if e == 1 else (0, 1), flat(turned[j % 4]))
+        last = 2 * E - 1
+        blocks_of_expert(E - 1, (0, 1), acc[last % 3][:])
+        for b in range(2):
+            nc.sync.dma_start(out[b * P : (b + 1) * P, :], windows[b][:])
+
+        last_block((1, 2), flat(turned[last % 4]))
+        last_block((3, 4), acc[last % 3][:])
+        last_block((5,), flat(turned[last % 4]))
+        scatter(2, C, 3 * C)
+        scatter(2, 3 * C, S)
+        nc.sync.dma_start(out[2 * P : 3 * P, :], windows[2][:])

@@ -32,6 +32,7 @@ def tile_moe_pkd_mlp_relu2_kernel(
     with ExitStack() as ctx:
         keep = ctx.enter_context(tc.tile_pool(name="keep", bufs=1))
         ring = ctx.enter_context(tc.tile_pool(name="ring", bufs=2))
+        early = ctx.enter_context(tc.tile_pool(name="early", bufs=1))
         psum = ctx.enter_context(tc.psum_pool(name="psum", bufs=1))
 
         offsets = keep.tile([P, S // 16], U16, name="offsets")
@@ -40,33 +41,35 @@ def tile_moe_pkd_mlp_relu2_kernel(
         def listed(a, b):
             return offsets[:, a // 16 : b // 16]
 
-        w1s = [keep.tile([P, (b - a) * PASSES, H], U8, name="w1s%d" % a, align_bytes=64) for a, b in W1_GROUPS[:2]]
-        xs = keep.tile([P, T], U8, name="xs", tag="xs", align_bytes=64)
-        planes = keep.tile([P, PASSES * S], U8, name="planes", align_bytes=64)
+        w1s = [keep.tile([P, PASSES, H], U8, name="w1s0", align_bytes=64)]
         w2s = keep.tile([P, E, N], U8, name="w2s", align_bytes=64)
+        xs = early.tile([P, T], U8, name="xs", align_bytes=64, offset=2048)
+        planes = keep.tile([P, PASSES * S], U8, name="planes", align_bytes=64)
         zero = keep.tile([P, 8], F32, name="zero")
 
         def clear(t):
             nc.vector.memset(t.bitcast(I32), 0)
 
+        nc.vector.memset(zero[:], 0.0)
         clear(xs[0:ROW0, :])
         clear(w1s[0][:])
-        nc.vector.memset(zero[:], 0.0)
         clear(planes[:])
-        clear(w1s[1][:])
         clear(w2s[:])
+        windows = {b: keep.tile([P, T], F32, name="window%d" % b) for b in range(2)}
+        nc.scalar.copy(windows[0][:], zero[:, 0:1].to_broadcast([P, T]))
 
         for o in range(PASSES):
             nc.sync.dma_start(xs[ROW0 + o : P : PASSES, :].bitcast(I32), x_scales[o].bitcast(I32))
-        xw = [keep.tile([P, T], U32, name="xw%d" % o, tag="xw%d" % o, align_bytes=64) for o in range(PASSES)]
+        xw = [early.tile([P, T], U32, name="xw0", align_bytes=64, offset=11264 + 2048)]
+        xw = xw + [keep.tile([P, T], U32, name="xw%d" % o, tag="xw%d" % o, align_bytes=64) for o in (1, 2)]
         for o in range(PASSES):
             nc.sync.dma_start(xw[o][:].bitcast(I32), x_words[o].rearrange("p t r -> p (t r)").bitcast(I32))
 
         w1 = {}
 
-        def load_w1(g, tag):
+        def load_w1(g, pool, **place):
             a, b = W1_GROUPS[g]
-            w1[g] = keep.tile([P, (b - a) * PASSES, 2 * H], U8, name="w1_%d" % g, tag=tag, align_bytes=64)
+            w1[g] = pool.tile([P, (b - a) * PASSES, 2 * H], U8, name="w1_%d" % g, align_bytes=64, **place)
             nc.sync.dma_start(w1[g][:].bitcast(I32), w1_words[a:b].rearrange("e s p c -> p (e s) c").bitcast(I32))
 
         def load_scales(tile, rows, queue):
@@ -78,14 +81,14 @@ def tile_moe_pkd_mlp_relu2_kernel(
             a, b = W1_GROUPS[g]
             load_scales(w1s[g], w1_scales[a + shift : b + shift], queue)
 
-        load_w1(0, "w1_first")
-        load_w1_scales(0, nc.gpsimd)
+        load_w1(0, keep)
+        load_w1_scales(0, nc.scalar)
+        load_scales(w2s, w2_scales, nc.sync)
+        nc.scalar.copy(windows[1][:], zero[:, 0:1].to_broadcast([P, T]))
         ident = keep.tile([P, P], F32, name="ident")
         make_identity(nc, ident[:])
-        load_w1_scales(1, nc.gpsimd)
-        load_scales(w2s, w2_scales, nc.gpsimd)
 
-        picked = keep.tile([P, S], U8, name="picked", tag="picked", align_bytes=64)
+        picked = keep.tile([P, S], U8, name="picked", align_bytes=64)
         nc.vector.tensor_copy(picked[:], xs[:].indirect(offsets[:]))
         for q in range(4):
             nc.scalar.dma_start(
@@ -93,14 +96,11 @@ def tile_moe_pkd_mlp_relu2_kernel(
                 picked[ROW0 + 12 * q : ROW0 + 12 * q + 12, :].bitcast(I32),
             )
 
-        load_w1(1, "xs")
-        w2 = keep.tile([P, E, 2 * N], U8, name="w2", tag="picked", align_bytes=64)
-        nc.sync.dma_start(w2[:].bitcast(I32), w2_words.rearrange("e s p c -> p (e s) c").bitcast(I32))
-
-        windows = [keep.tile([P, T], F32, name="window%d" % b) for b in range(BLOCKS)]
-        for b in range(BLOCKS):
-            nc.scalar.copy(windows[b][:], zero[:, 0:1].to_broadcast([P, T]))
-
+        w1s.append(early.tile([P, 2 * PASSES, H], U8, name="w1s1", align_bytes=64, offset=0))
+        clear(w1s[1][:])
+        load_w1_scales(1, nc.sync)
+        windows[2] = early.tile([P, T], F32, name="window2", align_bytes=64, offset=3072)
+        nc.scalar.copy(windows[2][:], zero[:, 0:1].to_broadcast([P, T]))
         words = {}
 
         def gather(tile, o, a, b):
@@ -111,20 +111,28 @@ def tile_moe_pkd_mlp_relu2_kernel(
         shared = keep.tile([P, 2 * C], U32, name="shared", align_bytes=64)
         g0 = keep.tile([P, S - C], U32, name="g0", align_bytes=64)
         g1a = keep.tile([P, C], U32, name="g1a", align_bytes=64)
-        g2a = keep.tile([P, C], U32, name="g2a", align_bytes=64)
+        g2a = keep.tile([P, C], U32, name="g2a", tag="g2a", align_bytes=64)
         g2 = keep.tile([P, S - C], U32, name="g2", align_bytes=64)
         gather(shared, 0, 0, C)
         gather(g0, 0, C, S)
-        gates = keep.tile([P, S], F32, name="gates", tag="xw0", align_bytes=64)
-        nc.sync.dma_start(gates[:], gate[0:P, :])
+        load_w1(1, early, offset=11264)
+        w2 = early.tile([P, E, 2 * N], U8, name="w2", align_bytes=64, offset=11264 + 7168)
+        nc.sync.dma_start(w2[:].bitcast(I32), w2_words.rearrange("e s p c -> p (e s) c").bitcast(I32))
+        gate_first = early.tile([P, C], F32, name="gate_first", align_bytes=64, offset=11264 + 6144)
+        nc.sync.dma_start(gate_first[:], gate[0:P, 0:C])
         gather(g1a, 1, 0, C)
         gather(g2a, 2, 0, C)
         gather(g2, 2, C, S)
-        load_w1(2, "xw2")
+        load_w1(2, keep, tag="xw2")
 
-        acc = [psum.tile([P, H], F32, name="acc%d" % n) for n in range(3)]
-        turned = [psum.tile([P, 4, P], F32, name="turned%d" % n) for n in range(4)]
-        early_bank = psum.tile([P, 2 * C], F32, name="early_bank")
+        banks = [psum.tile([P, H], F32, name="bank%d" % n) for n in range(6)]
+
+        def sums_bank(j):
+            return banks[j if j < 2 else 2 + j % 2][:]
+
+        def turned_bank(j):
+            return banks[2 + j if j < 2 else (4, 5, 0, 1)[(j - 2) % 4]][:]
+
         codes = keep.tile([P, S], U32, name="codes", align_bytes=64)
         hs = keep.tile([P, S], U8, name="hs", align_bytes=64)
         ys = keep.tile([P, BLOCKS, S], F32, name="ys")
@@ -138,7 +146,7 @@ def tile_moe_pkd_mlp_relu2_kernel(
             order = (2, 0, 1)
             for n, o in enumerate(order):
                 nc.tensor.matmul_mx(
-                    out=acc[j % 3][:],
+                    out=sums_bank(j),
                     lhsT=words[(o, j)].bitcast(FP8X4),
                     lhsT_scale=planes[:, o * S + j * P : o * S + (j + 1) * P],
                     rhs=w1[g][:, (e - first) * PASSES + o, :].bitcast(FP4X4),
@@ -147,7 +155,7 @@ def tile_moe_pkd_mlp_relu2_kernel(
                     stop=(n == PASSES - 1),
                 )
             relu[j] = ring.tile([P, 4, P], F32, name="relu", bufs=3)
-            nc.scalar.activation(relu[j][:], acc[j % 3][:].rearrange("p (m t) -> p t m", t=4), ACT.Relu)
+            nc.scalar.activation(relu[j][:], sums_bank(j).rearrange("p (m t) -> p t m", t=4), ACT.Relu)
 
         def turn(j):
             e = j // 2
@@ -157,10 +165,10 @@ def tile_moe_pkd_mlp_relu2_kernel(
                 else:
                     hidden[e] = ring.tile([P, C, 4], BF16, name="hidden", align_bytes=64)
             for t in range(4):
-                nc.tensor.transpose(turned[j % 4][:, t, :], relu[j][:, t, :], ident[:])
+                nc.tensor.transpose(turned_bank(j)[:, t * P : (t + 1) * P], relu[j][:, t, :], ident[:])
             half = (j % 2) * P
             nc.scalar.activation(
-                hidden[e][:, half : half + P, :], turned[j % 4][:].rearrange("p t s -> p s t"), ACT.Square
+                hidden[e][:, half : half + P, :], turned_bank(j).rearrange("p (t s) -> p s t", t=4), ACT.Square
             )
 
         def quantise(e):
@@ -170,26 +178,24 @@ def tile_moe_pkd_mlp_relu2_kernel(
                 in_=hidden[e][:].rearrange("p s t -> p (s t)"),
             )
 
-        def second_matmul(e, b, bank):
+        def second_matmul(e, b, bank, lo, hi):
             nc.tensor.matmul_mx(
                 out=bank,
                 lhsT=w2[:, e, 2 * b * P : 2 * (b + 1) * P].bitcast(FP4X4),
                 lhsT_scale=w2s[:, e, b * P : (b + 1) * P],
-                rhs=codes[:, e * C : (e + 1) * C].bitcast(FP8X4),
-                rhs_scale=hs[:, e * C : (e + 1) * C],
+                rhs=codes[:, lo:hi].bitcast(FP8X4),
+                rhs_scale=hs[:, lo:hi],
                 start=True,
                 stop=True,
             )
 
         def scatter(b, lo, hi):
-            nc.vector.tensor_tensor(windows[b][:].indirect(listed(lo, hi)), ys[:, b, lo:hi], gates[:, lo:hi], MULT)
-
-        def flat(bank):
-            return bank[:].rearrange("p t s -> p (t s)")
+            factor = gate_first[:] if lo == 0 else gate_rest[:, lo - C : hi - C]
+            nc.vector.tensor_tensor(windows[b][:].indirect(listed(lo, hi)), ys[:, b, lo:hi], factor, MULT)
 
         def blocks_of_expert(e, blocks, bank):
             for u, b in enumerate(blocks):
-                second_matmul(e, b, bank[:, u * C : (u + 1) * C])
+                second_matmul(e, b, bank[:, u * C : (u + 1) * C], e * C, (e + 1) * C)
             nc.scalar.copy(
                 ys[:, blocks[0] : blocks[-1] + 1, e * C : (e + 1) * C],
                 bank[:, 0 : len(blocks) * C].rearrange("p (u c) -> p u c", c=C),
@@ -197,14 +203,22 @@ def tile_moe_pkd_mlp_relu2_kernel(
             for b in blocks:
                 scatter(b, e * C, (e + 1) * C)
 
+        def first_expert_block(b, pair):
+            for u, bank in enumerate(pair):
+                second_matmul(0, b, bank[:, 0:P], u * P, (u + 1) * P)
+                nc.scalar.copy(ys[:, b, u * P : (u + 1) * P], bank[:, 0:P])
+            scatter(b, 0, C)
+
         def last_block(experts, bank):
             for u, e in enumerate(experts):
-                second_matmul(e, 2, bank[:, u * C : (u + 1) * C])
+                second_matmul(e, 2, bank[:, u * C : (u + 1) * C], e * C, (e + 1) * C)
             nc.scalar.copy(ys[:, 2, experts[0] * C : (experts[-1] + 1) * C], bank[:, 0 : len(experts) * C])
 
         first_layer(0)
         first_layer(1)
         gather(shared, 1, C, 3 * C)
+        gate_rest = keep.tile([P, S - C], F32, name="gate_rest", tag="g2a", align_bytes=64)
+        nc.sync.dma_start(gate_rest[:], gate[0:P, C:S])
         load_w1_scales(0, nc.sync, 3)
         for j in range(2 * E):
             turn(j)
@@ -217,19 +231,20 @@ def tile_moe_pkd_mlp_relu2_kernel(
             if j + 2 == 5:
                 load_w1_scales(1, nc.sync, 3)
             if j == 1:
-                blocks_of_expert(0, (0,), early_bank[:])
+                first_expert_block(0, (turned_bank(2), turned_bank(3)))
+                first_expert_block(1, (sums_bank(4), sums_bank(5)))
             elif j % 2 == 1:
                 e = j // 2
                 quantise(e)
-                blocks_of_expert(e - 1, (1, 2) if e == 1 else (0, 1), flat(turned[j % 4]))
+                blocks_of_expert(e - 1, (2,) if e == 1 else (0, 1), turned_bank(j))
         last = 2 * E - 1
-        blocks_of_expert(E - 1, (0, 1), acc[last % 3][:])
+        blocks_of_expert(E - 1, (0, 1), sums_bank(last))
         for b in range(2):
             nc.sync.dma_start(out[b * P : (b + 1) * P, :], windows[b][:])
 
-        last_block((1, 2), flat(turned[last % 4]))
-        last_block((3, 4), acc[last % 3][:])
-        last_block((5,), flat(turned[last % 4]))
+        last_block((1, 2), turned_bank(last))
+        last_block((3, 4), sums_bank(last))
+        last_block((5,), turned_bank(last))
         scatter(2, C, 3 * C)
         scatter(2, 3 * C, S)
         nc.sync.dma_start(out[2 * P : 3 * P, :], windows[2][:])

@@ -7,7 +7,7 @@ K, T, E, C, H, N = 1536, 2048, 6, 256, 512, 384
 S = E * C
 P = 128
 PASSES = K // 512
-BLOCKS = N // P
+TILES = S // P
 FLOPS = 2 * S * (K * H + H * N)
 
 F32 = mybir.dt.float32
@@ -22,7 +22,16 @@ ACT = mybir.ActivationFunctionType
 MULT = mybir.AluOpType.mult
 
 ROW0 = P - 16 * PASSES
+QUADRANT_ROWS = 4 * PASSES
+
 W1_GROUPS = ((0, 1), (1, 3), (3, 6))
+PLANE_REUSE = 3
+EARLY_EXPERTS = 2
+WARM_UP_PASSES = 6
+
+AT_PLANES_1, AT_X_SCALES, AT_WINDOW_2 = 0, 2048, 3072
+AT_W1_GROUP_1 = AT_WINDOW_2 + 8192
+AT_X_PASS_0, AT_GATE_FIRST, AT_W2 = AT_W1_GROUP_1 + 2048, AT_W1_GROUP_1 + 6144, AT_W1_GROUP_1 + 7168
 
 
 def tile_moe_pkd_mlp_relu2_kernel(
@@ -32,100 +41,110 @@ def tile_moe_pkd_mlp_relu2_kernel(
     with ExitStack() as ctx:
         keep = ctx.enter_context(tc.tile_pool(name="keep", bufs=1))
         ring = ctx.enter_context(tc.tile_pool(name="ring", bufs=2))
-        early = ctx.enter_context(tc.tile_pool(name="early", bufs=1))
+        overlay = ctx.enter_context(tc.tile_pool(name="overlay", bufs=1))
         psum = ctx.enter_context(tc.psum_pool(name="psum", bufs=1))
 
         offsets = keep.tile([P, S // 16], U16, name="offsets")
         nc.sync.dma_start(offsets[:], offs)
 
-        def listed(a, b):
-            return offsets[:, a // 16 : b // 16]
+        def listed(lo, hi):
+            return offsets[:, lo // 16 : hi // 16]
 
-        w1s = [keep.tile([P, PASSES, H], U8, name="w1s0", align_bytes=64)]
-        w2s = keep.tile([P, E, N], U8, name="w2s", align_bytes=64)
-        xs = early.tile([P, T], U8, name="xs", align_bytes=64, offset=2048)
-        planes = keep.tile([P, PASSES * S], U8, name="planes", align_bytes=64)
-        zero = keep.tile([P, 8], F32, name="zero")
+        w1_planes = [keep.tile([P, PASSES, H], U8, name="w1_planes0", align_bytes=64)]
+        w2_planes = keep.tile([P, E, N], U8, name="w2_planes", align_bytes=64)
+        x_rows = overlay.tile([P, T], U8, name="x_rows", align_bytes=64, offset=AT_X_SCALES)
+        slot_planes = keep.tile([P, PASSES * S], U8, name="slot_planes", align_bytes=64)
+        zero = keep.tile([P, 1], F32, name="zero")
 
-        def clear(t):
-            nc.vector.memset(t.bitcast(I32), 0)
+        def clear(view):
+            nc.vector.memset(view.bitcast(I32), 0)
+
+        def zero_window(window):
+            nc.scalar.copy(window[:], zero[:].to_broadcast([P, T]))
 
         nc.vector.memset(zero[:], 0.0)
-        clear(xs[0:ROW0, :])
-        clear(w1s[0][:])
-        clear(planes[:])
-        clear(w2s[:])
+        clear(x_rows[0:ROW0, :])
+        clear(w1_planes[0][:])
+        clear(slot_planes[:])
+        clear(w2_planes[:])
         windows = {b: keep.tile([P, T], F32, name="window%d" % b) for b in range(2)}
-        nc.scalar.copy(windows[0][:], zero[:, 0:1].to_broadcast([P, T]))
+        zero_window(windows[0])
 
         for o in range(PASSES):
-            nc.sync.dma_start(xs[ROW0 + o : P : PASSES, :].bitcast(I32), x_scales[o].bitcast(I32))
-        xw = [early.tile([P, T], U32, name="xw0", align_bytes=64, offset=11264 + 2048)]
-        xw = xw + [keep.tile([P, T], U32, name="xw%d" % o, tag="xw%d" % o, align_bytes=64) for o in (1, 2)]
-        for o in range(PASSES):
-            nc.sync.dma_start(xw[o][:].bitcast(I32), x_words[o].rearrange("p t r -> p (t r)").bitcast(I32))
-
+            nc.sync.dma_start(x_rows[ROW0 + o : P : PASSES, :].bitcast(I32), x_scales[o].bitcast(I32))
+        tokens = [overlay.tile([P, T], U32, name="tokens0", align_bytes=64, offset=AT_X_PASS_0)]
+        tokens = tokens + [
+            keep.tile([P, T], U32, name="tokens%d" % o, tag="tokens%d" % o, align_bytes=64) for o in (1, 2)
+        ]
         w1 = {}
 
-        def load_w1(g, pool, **place):
-            a, b = W1_GROUPS[g]
-            w1[g] = pool.tile([P, (b - a) * PASSES, 2 * H], U8, name="w1_%d" % g, align_bytes=64, **place)
-            nc.sync.dma_start(w1[g][:].bitcast(I32), w1_words[a:b].rearrange("e s p c -> p (e s) c").bitcast(I32))
+        def load_tokens(o):
+            nc.sync.dma_start(tokens[o][:].bitcast(I32), x_words[o].rearrange("p t r -> p (t r)").bitcast(I32))
 
-        def load_scales(tile, rows, queue):
+        def load_w1(g, pool, **place):
+            first, end = W1_GROUPS[g]
+            w1[g] = pool.tile([P, (end - first) * PASSES, 2 * H], U8, name="w1_%d" % g, align_bytes=64, **place)
+            words = w1_words[first:end].rearrange("e s p c -> p (e s) c")
+            nc.sync.dma_start(w1[g][:].bitcast(I32), words.bitcast(I32))
+
+        def load_planes(planes, rows, queue):
             by_row = rows.rearrange("e s (q r) i -> r q (e s) i", r=4)
             for r in range(4):
-                queue.dma_start(tile[r:P:32, :, :].bitcast(I32), by_row[r].bitcast(I32))
+                queue.dma_start(planes[r:P:32, :, :].bitcast(I32), by_row[r].bitcast(I32))
 
-        def load_w1_scales(g, queue, shift=0):
-            a, b = W1_GROUPS[g]
-            load_scales(w1s[g], w1_scales[a + shift : b + shift], queue)
+        def load_w1_planes(g, queue, shift=0):
+            first, end = W1_GROUPS[g]
+            load_planes(w1_planes[g], w1_scales[first + shift : end + shift], queue)
 
+        load_tokens(0)
+        load_tokens(1)
         load_w1(0, keep)
-        load_w1_scales(0, nc.scalar)
-        load_scales(w2s, w2_scales, nc.sync)
-        nc.scalar.copy(windows[1][:], zero[:, 0:1].to_broadcast([P, T]))
-        ident = keep.tile([P, P], F32, name="ident")
-        make_identity(nc, ident[:])
+        load_tokens(2)
+        load_w1_planes(0, nc.scalar)
+        load_planes(w2_planes, w2_scales, nc.sync)
+        zero_window(windows[1])
+        identity = keep.tile([P, P], F32, name="identity")
+        make_identity(nc, identity[:])
 
-        picked = keep.tile([P, S], U8, name="picked", align_bytes=64)
-        nc.vector.tensor_copy(picked[:], xs[:].indirect(offsets[:]))
+        slot_rows = keep.tile([P, S], U8, name="slot_rows", align_bytes=64)
+        nc.vector.tensor_copy(slot_rows[:], x_rows[:].indirect(offsets[:]))
         for q in range(4):
-            nc.scalar.dma_start(
-                planes[32 * q : 32 * q + 4, :].bitcast(I32),
-                picked[ROW0 + 12 * q : ROW0 + 12 * q + 12, :].bitcast(I32),
-            )
+            rows = slot_rows[ROW0 + QUADRANT_ROWS * q : ROW0 + QUADRANT_ROWS * (q + 1), :]
+            nc.scalar.dma_start(slot_planes[32 * q : 32 * q + 4, :].bitcast(I32), rows.bitcast(I32))
 
-        w1s.append(early.tile([P, 2 * PASSES, H], U8, name="w1s1", align_bytes=64, offset=0))
-        clear(w1s[1][:])
-        load_w1_scales(1, nc.sync)
-        windows[2] = early.tile([P, T], F32, name="window2", align_bytes=64, offset=3072)
-        nc.scalar.copy(windows[2][:], zero[:, 0:1].to_broadcast([P, T]))
-        words = {}
+        w1_planes.append(
+            overlay.tile([P, 2 * PASSES, H], U8, name="w1_planes1", align_bytes=64, offset=AT_PLANES_1)
+        )
+        clear(w1_planes[1][:])
+        load_w1_planes(1, nc.sync)
+        windows[2] = overlay.tile([P, T], F32, name="window2", align_bytes=64, offset=AT_WINDOW_2)
+        zero_window(windows[2])
 
-        def gather(tile, o, a, b):
-            nc.vector.tensor_copy(tile[:, 0 : b - a], xw[o][:].indirect(listed(a, b)))
-            for j in range(a // P, b // P):
-                words[(o, j)] = tile[:, j * P - a : (j + 1) * P - a]
+        slot_words = {}
 
-        shared = keep.tile([P, 2 * C], U32, name="shared", align_bytes=64)
-        g0 = keep.tile([P, S - C], U32, name="g0", align_bytes=64)
-        g1a = keep.tile([P, C], U32, name="g1a", align_bytes=64)
-        g2a = keep.tile([P, C], U32, name="g2a", tag="g2a", align_bytes=64)
-        g2 = keep.tile([P, S - C], U32, name="g2", align_bytes=64)
-        gather(shared, 0, 0, C)
-        gather(g0, 0, C, S)
-        load_w1(1, early, offset=11264)
-        w2 = early.tile([P, E, 2 * N], U8, name="w2", align_bytes=64, offset=11264 + 7168)
+        def gather(into, o, lo, hi):
+            nc.vector.tensor_copy(into[:, 0 : hi - lo], tokens[o][:].indirect(listed(lo, hi)))
+            for j in range(lo // P, hi // P):
+                slot_words[(o, j)] = into[:, j * P - lo : (j + 1) * P - lo]
+
+        reused = keep.tile([P, 2 * C], U32, name="reused", align_bytes=64)
+        pass0_rest = keep.tile([P, S - C], U32, name="pass0_rest", align_bytes=64)
+        pass1_first = keep.tile([P, C], U32, name="pass1_first", align_bytes=64)
+        pass2_first = keep.tile([P, C], U32, name="pass2_first", tag="pass2_first", align_bytes=64)
+        pass2_rest = keep.tile([P, S - C], U32, name="pass2_rest", align_bytes=64)
+        gather(reused, 0, 0, C)
+        gather(pass0_rest, 0, C, S)
+        load_w1(1, overlay, offset=AT_W1_GROUP_1)
+        w2 = overlay.tile([P, E, 2 * N], U8, name="w2", align_bytes=64, offset=AT_W2)
         nc.sync.dma_start(w2[:].bitcast(I32), w2_words.rearrange("e s p c -> p (e s) c").bitcast(I32))
-        gate_first = early.tile([P, C], F32, name="gate_first", align_bytes=64, offset=11264 + 6144)
+        gate_first = overlay.tile([P, C], F32, name="gate_first", align_bytes=64, offset=AT_GATE_FIRST)
         nc.sync.dma_start(gate_first[:], gate[0:P, 0:C])
-        gather(g1a, 1, 0, C)
-        gather(g2a, 2, 0, C)
-        gather(g2, 2, C, S)
-        load_w1(2, keep, tag="xw2")
+        gather(pass1_first, 1, 0, C)
+        gather(pass2_first, 2, 0, C)
+        gather(pass2_rest, 2, C, S)
+        load_w1(2, keep, tag="tokens2")
 
-        banks = [psum.tile([P, H], F32, name="bank%d" % n) for n in range(6)]
+        banks = [psum.tile([P, H], F32, name="bank%d" % n) for n in range(7)]
 
         def sums_bank(j):
             return banks[j if j < 2 else 2 + j % 2][:]
@@ -133,24 +152,23 @@ def tile_moe_pkd_mlp_relu2_kernel(
         def turned_bank(j):
             return banks[2 + j if j < 2 else (4, 5, 0, 1)[(j - 2) % 4]][:]
 
-        codes = keep.tile([P, S], U32, name="codes", align_bytes=64)
-        hs = keep.tile([P, S], U8, name="hs", align_bytes=64)
-        ys = keep.tile([P, BLOCKS, S], F32, name="ys")
+        h_words = keep.tile([P, S], U32, name="h_words", align_bytes=64)
+        h_plane = keep.tile([P, S], U8, name="h_plane", align_bytes=64)
+        y = keep.tile([P, N // P, S], F32, name="y")
         relu = {}
         hidden = {}
 
         def first_layer(j):
             e = j // 2
-            g = [n for n, (a, b) in enumerate(W1_GROUPS) if a <= e < b][0]
-            first = W1_GROUPS[g][0]
-            order = (2, 0, 1)
-            for n, o in enumerate(order):
+            g = [n for n, (first, end) in enumerate(W1_GROUPS) if first <= e < end][0]
+            place = e % PLANE_REUSE
+            for n, o in enumerate((2, 0, 1)):
                 nc.tensor.matmul_mx(
                     out=sums_bank(j),
-                    lhsT=words[(o, j)].bitcast(FP8X4),
-                    lhsT_scale=planes[:, o * S + j * P : o * S + (j + 1) * P],
-                    rhs=w1[g][:, (e - first) * PASSES + o, :].bitcast(FP4X4),
-                    rhs_scale=w1s[min(e % 3, 1)][:, max(e % 3 - 1, 0) * PASSES + o, :],
+                    lhsT=slot_words[(o, j)].bitcast(FP8X4),
+                    lhsT_scale=slot_planes[:, o * S + j * P : o * S + (j + 1) * P],
+                    rhs=w1[g][:, (e - W1_GROUPS[g][0]) * PASSES + o, :].bitcast(FP4X4),
+                    rhs_scale=w1_planes[min(place, 1)][:, max(place - 1, 0) * PASSES + o, :],
                     start=(n == 0),
                     stop=(n == PASSES - 1),
                 )
@@ -159,13 +177,12 @@ def tile_moe_pkd_mlp_relu2_kernel(
 
         def turn(j):
             e = j // 2
-            if j % 2 == 0:
-                if e == 0:
-                    hidden[e] = keep.tile([P, C, 4], BF16, name="hidden0", tag="handover", align_bytes=64)
-                else:
-                    hidden[e] = ring.tile([P, C, 4], BF16, name="hidden", align_bytes=64)
+            if j == 0:
+                hidden[e] = keep.tile([P, C, 4], BF16, name="hidden0", tag="handover", align_bytes=64)
+            elif j % 2 == 0:
+                hidden[e] = ring.tile([P, C, 4], BF16, name="hidden", align_bytes=64)
             for t in range(4):
-                nc.tensor.transpose(turned_bank(j)[:, t * P : (t + 1) * P], relu[j][:, t, :], ident[:])
+                nc.tensor.transpose(turned_bank(j)[:, t * P : (t + 1) * P], relu[j][:, t, :], identity[:])
             half = (j % 2) * P
             nc.scalar.activation(
                 hidden[e][:, half : half + P, :], turned_bank(j).rearrange("p (t s) -> p s t", t=4), ACT.Square
@@ -173,78 +190,81 @@ def tile_moe_pkd_mlp_relu2_kernel(
 
         def quantise(e):
             nc.vector.quantize_mx(
-                out=codes[:, e * C : (e + 1) * C].bitcast(FP8X4),
-                scales=hs[:, e * C : (e + 1) * C],
+                out=h_words[:, e * C : (e + 1) * C].bitcast(FP8X4),
+                scales=h_plane[:, e * C : (e + 1) * C],
                 in_=hidden[e][:].rearrange("p s t -> p (s t)"),
             )
 
-        def second_matmul(e, b, bank, lo, hi):
+        def second_layer(e, b, sums):
             nc.tensor.matmul_mx(
-                out=bank,
+                out=sums,
                 lhsT=w2[:, e, 2 * b * P : 2 * (b + 1) * P].bitcast(FP4X4),
-                lhsT_scale=w2s[:, e, b * P : (b + 1) * P],
-                rhs=codes[:, lo:hi].bitcast(FP8X4),
-                rhs_scale=hs[:, lo:hi],
+                lhsT_scale=w2_planes[:, e, b * P : (b + 1) * P],
+                rhs=h_words[:, e * C : (e + 1) * C].bitcast(FP8X4),
+                rhs_scale=h_plane[:, e * C : (e + 1) * C],
                 start=True,
                 stop=True,
             )
 
         def scatter(b, lo, hi):
             factor = gate_first[:] if lo == 0 else gate_rest[:, lo - C : hi - C]
-            nc.vector.tensor_tensor(windows[b][:].indirect(listed(lo, hi)), ys[:, b, lo:hi], factor, MULT)
+            nc.vector.tensor_tensor(windows[b][:].indirect(listed(lo, hi)), y[:, b, lo:hi], factor, MULT)
 
         def blocks_of_expert(e, blocks, bank):
             for u, b in enumerate(blocks):
-                second_matmul(e, b, bank[:, u * C : (u + 1) * C], e * C, (e + 1) * C)
+                second_layer(e, b, bank[:, u * C : (u + 1) * C])
             nc.scalar.copy(
-                ys[:, blocks[0] : blocks[-1] + 1, e * C : (e + 1) * C],
+                y[:, blocks[0] : blocks[-1] + 1, e * C : (e + 1) * C],
                 bank[:, 0 : len(blocks) * C].rearrange("p (u c) -> p u c", c=C),
             )
             for b in blocks:
                 scatter(b, e * C, (e + 1) * C)
 
-        def first_expert_block(b, pair):
-            for u, bank in enumerate(pair):
-                second_matmul(0, b, bank[:, 0:P], u * P, (u + 1) * P)
-                nc.scalar.copy(ys[:, b, u * P : (u + 1) * P], bank[:, 0:P])
-            scatter(b, 0, C)
+        def block_2_of_pair(e, bank):
+            for u in range(2):
+                second_layer(e + u, 2, bank[:, u * C : (u + 1) * C])
+            nc.scalar.copy(y[:, 2, e * C : (e + 2) * C], bank)
 
-        def last_block(experts, bank):
-            for u, e in enumerate(experts):
-                second_matmul(e, 2, bank[:, u * C : (u + 1) * C], e * C, (e + 1) * C)
-            nc.scalar.copy(ys[:, 2, experts[0] * C : (experts[-1] + 1) * C], bank[:, 0 : len(experts) * C])
+        for n in range(WARM_UP_PASSES):
+            nc.tensor.matmul_mx(
+                out=banks[6][:],
+                lhsT=slot_words[(0, 0)].bitcast(FP8X4),
+                lhsT_scale=slot_rows[:, 0:P],
+                rhs=w1[0][:, 0, :].bitcast(FP4X4),
+                rhs_scale=w1_planes[0][:, 0, :],
+                start=True,
+                stop=True,
+            )
 
         first_layer(0)
         first_layer(1)
-        gather(shared, 1, C, 3 * C)
-        gate_rest = keep.tile([P, S - C], F32, name="gate_rest", tag="g2a", align_bytes=64)
+        gather(reused, 1, C, 3 * C)
+        gate_rest = keep.tile([P, S - C], F32, name="gate_rest", tag="pass2_first", align_bytes=64)
         nc.sync.dma_start(gate_rest[:], gate[0:P, C:S])
-        load_w1_scales(0, nc.sync, 3)
-        for j in range(2 * E):
+        load_w1_planes(0, nc.sync, PLANE_REUSE)
+        for j in range(TILES):
             turn(j)
             if j == 1:
                 quantise(0)
-                g1c = keep.tile([P, 3 * C], U32, name="g1c", tag="handover", align_bytes=64)
-                gather(g1c, 1, 3 * C, S)
-            if j + 2 < 2 * E:
+                pass1_last = keep.tile([P, 3 * C], U32, name="pass1_last", tag="handover", align_bytes=64)
+                gather(pass1_last, 1, 3 * C, S)
+            if j + 2 < TILES:
                 first_layer(j + 2)
-            if j + 2 == 5:
-                load_w1_scales(1, nc.sync, 3)
-            if j == 1:
-                first_expert_block(0, (turned_bank(2), turned_bank(3)))
-                first_expert_block(1, (sums_bank(4), sums_bank(5)))
-            elif j % 2 == 1:
+            if j + 2 == 2 * PLANE_REUSE - 1:
+                load_w1_planes(1, nc.sync, PLANE_REUSE)
+            if j % 2 == 1:
                 e = j // 2
-                quantise(e)
-                blocks_of_expert(e - 1, (2,) if e == 1 else (0, 1), turned_bank(j))
-        last = 2 * E - 1
+                if e > 0:
+                    quantise(e)
+                    blocks_of_expert(e - 1, (0, 1), turned_bank(j))
+                if e < EARLY_EXPERTS:
+                    blocks_of_expert(e, (2,), turned_bank(j + 2))
+        last = TILES - 1
         blocks_of_expert(E - 1, (0, 1), sums_bank(last))
+
         for b in range(2):
             nc.sync.dma_start(out[b * P : (b + 1) * P, :], windows[b][:])
-
-        last_block((1, 2), turned_bank(last))
-        last_block((3, 4), sums_bank(last))
-        last_block((5,), turned_bank(last))
-        scatter(2, C, 3 * C)
-        scatter(2, 3 * C, S)
+        block_2_of_pair(EARLY_EXPERTS, turned_bank(last))
+        block_2_of_pair(EARLY_EXPERTS + 2, sums_bank(last))
+        scatter(2, EARLY_EXPERTS * C, S)
         nc.sync.dma_start(out[2 * P : 3 * P, :], windows[2][:])

from contextlib import ExitStack

import concourse.mybir as mybir
from concourse.masks import make_identity

K, T, E, C, H, N = 1536, 2048, 6, 256, 512, 384
S = E * C
P = 128
PASSES = K // 512
TILES = S // P
FLOPS = 2 * S * (K * H + H * N)

F32 = mybir.dt.float32
BF16 = mybir.dt.bfloat16
I32 = mybir.dt.int32
U32 = mybir.dt.uint32
U16 = mybir.dt.uint16
U8 = mybir.dt.uint8
FP8X4 = mybir.dt.float8_e4m3fn_x4
FP4X4 = mybir.dt.float4_e2m1fn_x4
ACT = mybir.ActivationFunctionType
MULT = mybir.AluOpType.mult

ROW0 = P - 16 * PASSES
QUADRANT_ROWS = 4 * PASSES

W1_GROUPS = ((0, 1), (1, 3), (3, 6))
PLANE_REUSE = 3
EARLY_EXPERTS = 2
WARM_UP_PASSES = 6

AT_PLANES_1, AT_X_SCALES, AT_WINDOW_2 = 0, 2048, 3072
AT_W1_GROUP_1 = AT_WINDOW_2 + 8192
AT_X_PASS_0, AT_GATE_FIRST, AT_W2 = AT_W1_GROUP_1 + 2048, AT_W1_GROUP_1 + 6144, AT_W1_GROUP_1 + 7168


def tile_moe_pkd_mlp_relu2_kernel(
    tc, x_words, x_scales, w1_words, w1_scales, w2_words, w2_scales, gate, offs, out
):
    nc = tc.nc
    with ExitStack() as ctx:
        keep = ctx.enter_context(tc.tile_pool(name="keep", bufs=1))
        ring = ctx.enter_context(tc.tile_pool(name="ring", bufs=2))
        overlay = ctx.enter_context(tc.tile_pool(name="overlay", bufs=1))
        psum = ctx.enter_context(tc.psum_pool(name="psum", bufs=1))

        offsets = keep.tile([P, S // 16], U16, name="offsets")
        nc.sync.dma_start(offsets[:], offs)

        def listed(lo, hi):
            return offsets[:, lo // 16 : hi // 16]

        w1_planes = [keep.tile([P, PASSES, H], U8, name="w1_planes0", align_bytes=64)]
        w2_planes = keep.tile([P, E, N], U8, name="w2_planes", align_bytes=64)
        x_rows = overlay.tile([P, T], U8, name="x_rows", align_bytes=64, offset=AT_X_SCALES)
        slot_planes = keep.tile([P, PASSES * S], U8, name="slot_planes", align_bytes=64)
        zero = keep.tile([P, 1], F32, name="zero")

        def clear(view):
            nc.vector.memset(view.bitcast(I32), 0)

        def zero_window(window):
            nc.scalar.copy(window[:], zero[:].to_broadcast([P, T]))

        nc.vector.memset(zero[:], 0.0)
        clear(x_rows[0:ROW0, :])
        clear(w1_planes[0][:])
        clear(slot_planes[:])
        clear(w2_planes[:])
        windows = {b: keep.tile([P, T], F32, name="window%d" % b) for b in range(2)}
        zero_window(windows[0])

        for o in range(PASSES):
            nc.sync.dma_start(x_rows[ROW0 + o : P : PASSES, :].bitcast(I32), x_scales[o].bitcast(I32))
        tokens = [overlay.tile([P, T], U32, name="tokens0", align_bytes=64, offset=AT_X_PASS_0)]
        tokens = tokens + [
            keep.tile([P, T], U32, name="tokens%d" % o, tag="tokens%d" % o, align_bytes=64) for o in (1, 2)
        ]
        w1 = {}

        def load_tokens(o):
            nc.sync.dma_start(tokens[o][:].bitcast(I32), x_words[o].rearrange("p t r -> p (t r)").bitcast(I32))

        def load_w1(g, pool, **place):
            first, end = W1_GROUPS[g]
            w1[g] = pool.tile([P, (end - first) * PASSES, 2 * H], U8, name="w1_%d" % g, align_bytes=64, **place)
            words = w1_words[first:end].rearrange("e s p c -> p (e s) c")
            nc.sync.dma_start(w1[g][:].bitcast(I32), words.bitcast(I32))

        def load_planes(planes, rows, queue):
            by_row = rows.rearrange("e s (q r) i -> r q (e s) i", r=4)
            for r in range(4):
                queue.dma_start(planes[r:P:32, :, :].bitcast(I32), by_row[r].bitcast(I32))

        def load_w1_planes(g, queue, shift=0):
            first, end = W1_GROUPS[g]
            load_planes(w1_planes[g], w1_scales[first + shift : end + shift], queue)

        load_tokens(0)
        load_tokens(1)
        load_w1(0, keep)
        load_tokens(2)
        load_w1_planes(0, nc.scalar)
        load_planes(w2_planes, w2_scales, nc.sync)
        zero_window(windows[1])
        identity = keep.tile([P, P], F32, name="identity")
        make_identity(nc, identity[:])

        slot_rows = keep.tile([P, S], U8, name="slot_rows", align_bytes=64)
        nc.vector.tensor_copy(slot_rows[:], x_rows[:].indirect(offsets[:]))
        for q in range(4):
            rows = slot_rows[ROW0 + QUADRANT_ROWS * q : ROW0 + QUADRANT_ROWS * (q + 1), :]
            nc.scalar.dma_start(slot_planes[32 * q : 32 * q + 4, :].bitcast(I32), rows.bitcast(I32))

        w1_planes.append(
            overlay.tile([P, 2 * PASSES, H], U8, name="w1_planes1", align_bytes=64, offset=AT_PLANES_1)
        )
        clear(w1_planes[1][:])
        load_w1_planes(1, nc.sync)
        windows[2] = overlay.tile([P, T], F32, name="window2", align_bytes=64, offset=AT_WINDOW_2)
        zero_window(windows[2])

        slot_words = {}

        def gather(into, o, lo, hi):
            nc.vector.tensor_copy(into[:, 0 : hi - lo], tokens[o][:].indirect(listed(lo, hi)))
            for j in range(lo // P, hi // P):
                slot_words[(o, j)] = into[:, j * P - lo : (j + 1) * P - lo]

        reused = keep.tile([P, 2 * C], U32, name="reused", align_bytes=64)
        pass0_rest = keep.tile([P, S - C], U32, name="pass0_rest", align_bytes=64)
        pass1_first = keep.tile([P, C], U32, name="pass1_first", align_bytes=64)
        pass2_first = keep.tile([P, C], U32, name="pass2_first", tag="pass2_first", align_bytes=64)
        pass2_rest = keep.tile([P, S - C], U32, name="pass2_rest", align_bytes=64)
        gather(reused, 0, 0, C)
        gather(pass0_rest, 0, C, S)
        load_w1(1, overlay, offset=AT_W1_GROUP_1)
        w2 = overlay.tile([P, E, 2 * N], U8, name="w2", align_bytes=64, offset=AT_W2)
        nc.sync.dma_start(w2[:].bitcast(I32), w2_words.rearrange("e s p c -> p (e s) c").bitcast(I32))
        gate_first = overlay.tile([P, C], F32, name="gate_first", align_bytes=64, offset=AT_GATE_FIRST)
        nc.sync.dma_start(gate_first[:], gate[0:P, 0:C])
        gather(pass1_first, 1, 0, C)
        gather(pass2_first, 2, 0, C)
        gather(pass2_rest, 2, C, S)
        load_w1(2, keep, tag="tokens2")

        banks = [psum.tile([P, H], F32, name="bank%d" % n) for n in range(7)]

        def sums_bank(j):
            return banks[j if j < 2 else 2 + j % 2][:]

        def turned_bank(j):
            return banks[2 + j if j < 2 else (4, 5, 0, 1)[(j - 2) % 4]][:]

        h_words = keep.tile([P, S], U32, name="h_words", align_bytes=64)
        h_plane = keep.tile([P, S], U8, name="h_plane", align_bytes=64)
        y = keep.tile([P, N // P, S], F32, name="y")
        relu = {}
        hidden = {}

        def first_layer(j):
            e = j // 2
            g = [n for n, (first, end) in enumerate(W1_GROUPS) if first <= e < end][0]
            place = e % PLANE_REUSE
            for n, o in enumerate((2, 0, 1)):
                nc.tensor.matmul_mx(
                    out=sums_bank(j),
                    lhsT=slot_words[(o, j)].bitcast(FP8X4),
                    lhsT_scale=slot_planes[:, o * S + j * P : o * S + (j + 1) * P],
                    rhs=w1[g][:, (e - W1_GROUPS[g][0]) * PASSES + o, :].bitcast(FP4X4),
                    rhs_scale=w1_planes[min(place, 1)][:, max(place - 1, 0) * PASSES + o, :],
                    start=(n == 0),
                    stop=(n == PASSES - 1),
                )
            relu[j] = ring.tile([P, 4, P], F32, name="relu", bufs=3)
            nc.scalar.activation(relu[j][:], sums_bank(j).rearrange("p (m t) -> p t m", t=4), ACT.Relu)

        def turn(j):
            e = j // 2
            if j == 0:
                hidden[e] = keep.tile([P, C, 4], BF16, name="hidden0", tag="handover", align_bytes=64)
            elif j % 2 == 0:
                hidden[e] = ring.tile([P, C, 4], BF16, name="hidden", align_bytes=64)
            for t in range(4):
                nc.tensor.transpose(turned_bank(j)[:, t * P : (t + 1) * P], relu[j][:, t, :], identity[:])
            half = (j % 2) * P
            nc.scalar.activation(
                hidden[e][:, half : half + P, :], turned_bank(j).rearrange("p (t s) -> p s t", t=4), ACT.Square
            )

        def quantise(e):
            nc.vector.quantize_mx(
                out=h_words[:, e * C : (e + 1) * C].bitcast(FP8X4),
                scales=h_plane[:, e * C : (e + 1) * C],
                in_=hidden[e][:].rearrange("p s t -> p (s t)"),
            )

        def second_layer(e, b, sums):
            nc.tensor.matmul_mx(
                out=sums,
                lhsT=w2[:, e, 2 * b * P : 2 * (b + 1) * P].bitcast(FP4X4),
                lhsT_scale=w2_planes[:, e, b * P : (b + 1) * P],
                rhs=h_words[:, e * C : (e + 1) * C].bitcast(FP8X4),
                rhs_scale=h_plane[:, e * C : (e + 1) * C],
                start=True,
                stop=True,
            )

        def scatter(b, lo, hi):
            factor = gate_first[:] if lo == 0 else gate_rest[:, lo - C : hi - C]
            nc.vector.tensor_tensor(windows[b][:].indirect(listed(lo, hi)), y[:, b, lo:hi], factor, MULT)

        def blocks_of_expert(e, blocks, bank):
            for u, b in enumerate(blocks):
                second_layer(e, b, bank[:, u * C : (u + 1) * C])
            nc.scalar.copy(
                y[:, blocks[0] : blocks[-1] + 1, e * C : (e + 1) * C],
                bank[:, 0 : len(blocks) * C].rearrange("p (u c) -> p u c", c=C),
            )
            for b in blocks:
                scatter(b, e * C, (e + 1) * C)

        def block_2_of_pair(e, bank):
            for u in range(2):
                second_layer(e + u, 2, bank[:, u * C : (u + 1) * C])
            nc.scalar.copy(y[:, 2, e * C : (e + 2) * C], bank)

        for n in range(WARM_UP_PASSES):
            nc.tensor.matmul_mx(
                out=banks[6][:],
                lhsT=slot_words[(0, 0)].bitcast(FP8X4),
                lhsT_scale=slot_rows[:, 0:P],
                rhs=w1[0][:, 0, :].bitcast(FP4X4),
                rhs_scale=w1_planes[0][:, 0, :],
                start=True,
                stop=True,
            )

        first_layer(0)
        first_layer(1)
        gather(reused, 1, C, 3 * C)
        gate_rest = keep.tile([P, S - C], F32, name="gate_rest", tag="pass2_first", align_bytes=64)
        nc.sync.dma_start(gate_rest[:], gate[0:P, C:S])
        load_w1_planes(0, nc.sync, PLANE_REUSE)
        for j in range(TILES):
            turn(j)
            if j == 1:
                quantise(0)
                pass1_last = keep.tile([P, 3 * C], U32, name="pass1_last", tag="handover", align_bytes=64)
                gather(pass1_last, 1, 3 * C, S)
            if j + 2 < TILES:
                first_layer(j + 2)
            if j + 2 == 2 * PLANE_REUSE - 1:
                load_w1_planes(1, nc.sync, PLANE_REUSE)
            if j % 2 == 1:
                e = j // 2
                if e > 0:
                    quantise(e)
                    blocks_of_expert(e - 1, (0, 1), turned_bank(j))
                if e < EARLY_EXPERTS:
                    blocks_of_expert(e, (2,), turned_bank(j + 2))
        last = TILES - 1
        blocks_of_expert(E - 1, (0, 1), sums_bank(last))

        for b in range(2):
            nc.sync.dma_start(out[b * P : (b + 1) * P, :], windows[b][:])
        block_2_of_pair(EARLY_EXPERTS, turned_bank(last))
        block_2_of_pair(EARLY_EXPERTS + 2, sums_bank(last))
        scatter(2, EARLY_EXPERTS * C, S)
        nc.sync.dma_start(out[2 * P : 3 * P, :], windows[2][:])
